import numpy as np
import ml_dtypes


def mxq(x, axis, fmt="e4m3"):
    dtype, down = {"e4m3": (ml_dtypes.float8_e4m3fn, 7), "e5m2": (ml_dtypes.float8_e5m2, 14)}[fmt]
    v = np.moveaxis(np.asarray(x, np.float32).astype(ml_dtypes.bfloat16).astype(np.float64), axis, -1)
    blocks = v.reshape(v.shape[:-1] + (-1, 32))
    amax = np.abs(blocks).max(-1, keepdims=True)
    byte = np.maximum(np.where(amax > 0, np.frexp(amax)[1] - 1 + 127, 0) - down, 1)
    scale = np.exp2(byte - 127.0)
    codes = (blocks / scale).astype(np.float32).astype(dtype).astype(np.float64)
    return np.moveaxis((codes * scale).reshape(v.shape), -1, axis)


WIDE = False


def mx_kscale(k):
    if not WIDE:
        return np.ones(k)
    levels = np.array([10, -10, 5, -5, 0])
    if k % 512:
        return np.exp2(np.random.permutation(np.resize(levels, k // 32))).repeat(32)
    a = np.empty((k // 512, 16))
    for p in range(k // 512):
        a[p, :8] = np.random.permutation(np.resize(levels, 8))
        for g in range(8):
            far = levels[np.abs(levels - a[p, g]) >= 10]
            a[p, g + 8] = far[np.random.randint(len(far))]
    return np.exp2(a.ravel()).repeat(32)


def f64(x):
    return np.asarray(x).astype(np.float64)


def striped(idx):
    return np.tile(idx.reshape(-1, 16).T, (8, 1)).astype(np.uint16)


def unstriped(offs):
    return offs[:16].T.reshape(-1).astype(np.int64)


def striped8(idx):
    return np.concatenate([x.reshape(-1, 16).T for x in idx]).astype(np.uint16)


def runs(offs, k):
    lists = np.stack([offs[16 * r : 16 * r + 16].T.reshape(-1) for r in range(8)]).astype(np.int64)
    return lists[np.arange(k) % 512 // 64]


def pack_weight(w):
    k, n = w.shape
    w = f64(np.asarray(w, np.float32).astype(ml_dtypes.bfloat16)).reshape(k // 32, 32, n)
    amax = np.abs(w).max(1)
    byte = np.clip(np.where(amax > 0, np.frexp(amax)[1] - 1 + 127 - 7, 1), 1, 254)
    scaled = (w * np.exp2(127.0 - byte)[:, None, :]).reshape(k, n).astype(np.float32)
    words = np.ascontiguousarray(scaled.reshape(k // 512, 128, 4, n).transpose(0, 1, 3, 2)).astype(ml_dtypes.float8_e4m3fn).view(np.uint8)
    return words, np.ascontiguousarray(byte.astype(np.uint8).reshape(k // 512, 16, n))


def unpack_weight(words, scales):
    g, p, n, _ = words.shape
    vals = np.ascontiguousarray(words).view(ml_dtypes.float8_e4m3fn).astype(np.float64) * np.repeat(np.exp2(scales.astype(np.float64) - 127.0), 8, axis=1)[..., None]
    return vals.transpose(0, 1, 3, 2).reshape(g * 512, n)


def sigmoid(v):
    return 1.0 / (1.0 + np.exp(-np.maximum(v, -700.0)))

def planes(y):
    n, m = y.shape
    v = y.astype(np.float32).astype(ml_dtypes.bfloat16).astype(np.float64).reshape(n // 32, 32, m)
    top = np.abs(v).max(1)
    byte = np.clip(np.where(top > 0, np.frexp(top)[1] - 1 + 127 - 7, 1), 1, 254)
    codes = (v * np.exp2(127.0 - byte)[:, None, :]).reshape(n, m).astype(np.float32).astype(ml_dtypes.float8_e4m3fn).view(np.uint8)
    words = codes.reshape(n // 512, 128, 4, m).transpose(0, 1, 3, 2)
    return np.ascontiguousarray(words), np.ascontiguousarray(byte.astype(np.uint8).reshape(n // 512, 16, m))


K, T, S, V, G, H, W = 512, 1024, 512, 512, 2048, 512, 256


def setup_inputs():
    n = np.random.standard_normal
    s = mx_kscale(K)[:, None]
    u = mx_kscale(S)
    packed_xT = pack_weight(n((K, T)) * s)
    packed_dT = pack_weight(n((K, G)) / s)
    packed_w1 = pack_weight(n((K, H)) / np.sqrt(K) / s)
    perm = np.stack([np.random.permutation(V) for _ in range(8)])
    return {
        "x_words": packed_xT[0],
        "x_scales": packed_xT[1],
        "d_words": packed_dT[0],
        "d_scales": packed_dT[1],
        "w1_words": packed_w1[0],
        "w1_scales": packed_w1[1],
        "ga": (np.random.uniform(0.5, 1.5, (H, 1)) * u[:, None]).astype(np.float32),
        "gb": (np.random.uniform(0.5, 1.5, (H, 1)) / u[:, None]).astype(np.float32),
        "offs": striped(np.random.permutation(T)[:S]),
        "k1": striped8(np.random.randint(0, G, (8, H))),
        "two": striped(np.random.permutation(T)[:V]),
        "n1": striped8(np.stack([np.random.permutation(S) for _ in range(8)])),
        "n2": striped8(np.stack([np.random.permutation(S) for _ in range(8)])),
        "n3": striped8(np.stack([np.random.permutation(V) for _ in range(8)])),
        "n4": striped8(np.stack([np.random.permutation(V) for _ in range(8)])),
        "n5": striped8(perm[:, :W]),
        "n6": striped8(perm[:, W:]),
    }


def reference(x_words, x_scales, d_words, d_scales, w1_words, w1_scales, ga, gb, offs, k1, two, n1, n2, n3, n4, n5, n6):
    d_k1 = unpack_weight(d_words, d_scales)[np.arange(K)[:, None], runs(k1, K)]
    xq = unpack_weight(x_words, x_scales)[:, unstriped(offs)]
    a = 0.0625 * (d_k1.T @ xq)
    z = f64(ga) * (a * (sigmoid(a[np.arange(H)[:, None], runs(n1, H)] - (a[np.arange(H)[:, None], runs(n2, H)]))))
    x_two = unpack_weight(x_words, x_scales)[:, unstriped(two)]
    b = unpack_weight(w1_words, w1_scales).T @ x_two
    z2 = f64(gb) * (np.minimum(np.maximum(b, b[np.arange(H)[:, None], runs(n3, H)]), b[np.arange(H)[:, None], runs(n4, H)]))
    s = 0.0625 * ((mxq(z, 0, "e4m3").T @ mxq(z2, 0, "e4m3")))
    pa = s[np.arange(S)[:, None], runs(n5, S)]
    pb = s[np.arange(S)[:, None], runs(n6, S)]
    rb = pa - pb
    ra = 0.75 * (pa + pb)
    ds = np.zeros((S, V))
    ds[np.arange(S)[:, None], runs(n5, S)] = ra
    out = ds.copy()
    out[np.arange(S)[:, None], runs(n6, S)] = rb
    return (out,) + planes(out)

@@ -1,0 +1,247 @@
+from contextlib import ExitStack
+
+import concourse.mybir as mybir
+
+F32 = mybir.dt.float32
+BF16 = mybir.dt.bfloat16
+I32 = mybir.dt.int32
+U32 = mybir.dt.uint32
+U16 = mybir.dt.uint16
+U8 = mybir.dt.uint8
+FP8X4 = mybir.dt.float8_e4m3fn_x4
+ALU = mybir.AluOpType
+ACT = mybir.ActivationFunctionType
+
+P = 128
+PACK = 4
+N = 512
+HALF = 256
+T = 1024
+G = 2048
+FLOPS = 3 * 2 * 512 * 512 * 512
+
+
+def as_words(dram):
+    return dram[0].rearrange("p n t -> p (n t)").bitcast(I32)
+
+
+def tile_picked_ckqcmpminmxhaar_none_po_kernel(
+    tc, x_words, x_scales, d_words, d_scales, w1_words, w1_scales, ga, gb,
+    offs, k1, two, n1, n2, n3, n4, n5, n6, out_0, out_1, out_2,
+):
+    nc = tc.nc
+    with ExitStack() as ctx:
+        keep = ctx.enter_context(tc.tile_pool(name="keep", bufs=1))
+        psum = ctx.enter_context(tc.psum_pool(name="psum", bufs=1))
+
+        def sb(name, shape, dtype):
+            return keep.tile(shape, dtype, name=name, align_bytes=64)
+
+        def load_list(name, dram):
+            tile = sb(name, list(dram.shape), U16)
+            nc.sync.dma_start(tile[:], dram)
+            return tile
+
+        def product(bank, lw, ls, rw, rs):
+            nc.tensor.matmul_mx(out=bank, lhsT=lw.bitcast(FP8X4), lhsT_scale=ls,
+                                rhs=rw.bitcast(FP8X4), rhs_scale=rs, start=True, stop=True)
+
+        ds_in = sb("ds_in", [P, G], U8)
+        xs_in = sb("xs_in", [P, T], U8)
+        ws_in = sb("ws_in", [P, N], U8)
+        ds_placed = sb("ds_placed", [P, N], U8)
+        nc.vector.memset(ds_in[:].bitcast(I32), 0)
+        nc.gpsimd.memset(xs_in[:].bitcast(I32), 0)
+        nc.gpsimd.memset(ws_in[:].bitcast(I32), 0)
+        nc.gpsimd.memset(ds_placed[:].bitcast(I32), 0)
+        warm = sb("warm", [P, 1], F32)
+        warm_out = sb("warm_out", [P, 1], F32)
+        nc.gpsimd.memset(warm[:], 0.0)
+        nc.scalar.activation(warm_out[:], warm[:], ACT.Sigmoid)
+        three_quarters = sb("three_quarters", [P, HALF], F32)
+        nc.gpsimd.memset(three_quarters[:], 0.75)
+
+        offs_l = load_list("offs_l", offs)
+        k1_l = load_list("k1_l", k1)
+        xw_in = sb("xw_in", [P, T], U32)
+        nc.sync.dma_start(xw_in[:].bitcast(I32), as_words(x_words))
+        nc.sync.dma_start(ds_in[:].bitcast(I32)[0:P:8, :], d_scales[0].bitcast(I32))
+        dw_in = sb("dw_in", [P, G], U32)
+        nc.sync.dma_start(dw_in[:].bitcast(I32), as_words(d_words))
+        for q in range(4):
+            nc.scalar.dma_start(xs_in[:].bitcast(I32)[32 * q : 32 * q + 4, :],
+                                x_scales[0].bitcast(I32)[4 * q : 4 * q + 4, :])
+        two_l = load_list("two_l", two)
+        ga_in = sb("ga_in", [P, PACK], F32)
+        gb_in = sb("gb_in", [P, PACK], F32)
+        nc.sync.dma_start(gb_in[:], gb.rearrange("(p t) o -> p (t o)", t=PACK))
+        nc.sync.dma_start(ga_in[:], ga.rearrange("(p t) o -> p (t o)", t=PACK))
+        n2_l = load_list("n2_l", n2)
+        n1_l = load_list("n1_l", n1)
+        ww_in = sb("ww_in", [P, N], U32)
+        nc.sync.dma_start(ww_in[:].bitcast(I32), as_words(w1_words))
+        for q in range(4):
+            nc.gpsimd.dma_start(ws_in[:].bitcast(I32)[32 * q : 32 * q + 4, :],
+                                w1_scales[0].bitcast(I32)[4 * q : 4 * q + 4, :])
+        n3_l = load_list("n3_l", n3)
+        n4_l = load_list("n4_l", n4)
+        n6_l = load_list("n6_l", n6)
+        n5_l = load_list("n5_l", n5)
+
+        twice_nonneg = sb("twice_nonneg", [P, PACK], F32)
+        sign = sb("sign", [P, PACK], F32)
+        sign16 = sb("sign16", [P, PACK], F32)
+        gb_abs = sb("gb_abs", [P, PACK], F32)
+        ga_signed = sb("ga_signed", [P, PACK], F32)
+        nc.gpsimd.tensor_scalar(twice_nonneg[:], gb_in[:], 0.0, 2.0, ALU.is_ge, ALU.mult)
+        nc.gpsimd.tensor_scalar(sign[:], twice_nonneg[:], 1.0, -1.0, ALU.mult, ALU.add)
+        nc.gpsimd.tensor_tensor(gb_abs[:], gb_in[:], sign[:], ALU.mult)
+        nc.gpsimd.tensor_scalar(sign16[:], twice_nonneg[:], 0.0625, -0.0625, ALU.mult, ALU.add)
+        nc.gpsimd.tensor_tensor(ga_signed[:], ga_in[:], sign16[:], ALU.mult)
+
+        ww = sb("ww", [P, N], U32)
+        ws = sb("ws", [P, N], U8)
+        nc.gpsimd.tensor_copy(ww[:].rearrange("p (t m) -> p t m", t=PACK), ww_in[:].rearrange("p (m t) -> p t m", t=PACK))
+        nc.gpsimd.tensor_copy(ws[:].rearrange("p (t m) -> p t m", t=PACK), ws_in[:].rearrange("p (m t) -> p t m", t=PACK))
+
+        x1w = sb("x1w", [P, N], U32)
+        nc.vector.tensor_copy(x1w[:], xw_in[:].indirect(offs_l[:]))
+        ds_got = sb("ds_got", [P, N], U8)
+        ds_dealt = sb("ds_dealt", [P, N], U8)
+        nc.vector.tensor_copy(ds_got[:], ds_in[:].indirect(k1_l[:]))
+        x1s = sb("x1s", [P, N], U8)
+        nc.vector.tensor_copy(ds_dealt[:].rearrange("p (t m) -> p m t", t=PACK), ds_got[:].rearrange("p (m t) -> p m t", t=PACK))
+        for q in range(4):
+            nc.scalar.dma_start(ds_placed[:].bitcast(I32)[32 * q : 32 * q + 4, :],
+                                ds_dealt[:].bitcast(I32)[32 * q : 32 * q + 32 : 8, :])
+        dw_got = sb("dw_got", [P, N], U32)
+        nc.vector.tensor_copy(dw_got[:], dw_in[:].indirect(k1_l[:]))
+        nc.vector.tensor_copy(x1s[:], xs_in[:].indirect(offs_l[:]))
+        dw = sb("dw", [P, N], U32)
+        nc.vector.tensor_copy(dw[:].rearrange("p (t m) -> p m t", t=PACK), dw_got[:].rearrange("p (m t) -> p m t", t=PACK))
+        x2w = sb("x2w", [P, N], U32)
+        nc.vector.tensor_copy(x2w[:], xw_in[:].indirect(two_l[:]))
+        x2s = sb("x2s", [P, N], U8)
+        nc.vector.tensor_copy(x2s[:], xs_in[:].indirect(two_l[:]))
+
+        a_rows = []
+        a_gained = sb("a_gained", [P, PACK, N], F32)
+        a_banks = []
+        for t in range(PACK):
+            bank = psum.tile([P, N], F32, name=f"a_bank{t}", tag=f"bank{4 + t}")
+            cols = slice(P * t, P * (t + 1))
+            product(bank[:], dw[:, cols], ds_placed[:, cols], x1w[:], x1s[:])
+            row = sb(f"a_row{t}", [P, 2 * N], F32)
+            nc.scalar.copy(row[:, 0:N], bank[:])
+            a_rows.append(row)
+            a_banks.append(bank)
+
+        b_rows = []
+        for t in range(PACK):
+            bank = psum.tile([P, N], F32, name=f"b_bank{t}", tag=f"bank{t}")
+            cols = slice(P * t, P * (t + 1))
+            product(bank[:], ww[:, cols], ws[:, cols], x2w[:], x2s[:])
+            row = sb(f"b_row{t}", [P, N], F32)
+            nc.scalar.activation(row[:], bank[:], ACT.Copy, scale=gb_abs[:, t : t + 1])
+            b_rows.append(row)
+
+        z2_bf = sb("z2_bf", [P, N, PACK], BF16)
+        z2w = sb("z2w", [P, N], U32)
+        z2s = sb("z2s", [P, N], U8)
+
+        def b_gather(h):
+            lists = slice(16 * h, 16 * (h + 1))
+            cols = slice(HALF * h, HALF * (h + 1))
+            at3 = sb(f"at3_{h}", [P, PACK, HALF], F32)
+            at4 = sb(f"at4_{h}", [P, PACK, HALF], F32)
+            larger = sb(f"larger{h}", [P, PACK, HALF], F32)
+            for t in range(PACK + 1):
+                if t < PACK:
+                    nc.vector.tensor_copy(at3[:, t, :], b_rows[t][:].indirect(n3_l[:, lists]))
+                if t > 0:
+                    nc.vector.tensor_copy(at4[:, t - 1, :], b_rows[t - 1][:].indirect(n4_l[:, lists]))
+                if t < PACK:
+                    nc.vector.tensor_tensor(larger[:, t, :], at3[:, t, :], b_rows[t][:, cols], ALU.max)
+            nc.vector.tensor_tensor(
+                z2_bf[:, cols, :].rearrange("p (c i) t -> p c t i", i=4),
+                larger[:].rearrange("p t (c i) -> p c t i", i=4),
+                at4[:].rearrange("p t (c i) -> p c t i", i=4),
+                ALU.min,
+            )
+
+        def b_quantize(h):
+            cols = slice(HALF * h, HALF * (h + 1))
+            nc.vector.quantize_mx(out=z2w[:, cols].bitcast(FP8X4), scales=z2s[:, cols],
+                                  in_=z2_bf[:, cols, :].rearrange("p n t -> p (n t)"))
+
+        gate = sb("gate", [P, PACK, N], F32)
+        at2 = [sb(f"at2_{t}", [P, N], F32) for t in range(PACK)]
+        nc.vector.tensor_copy(at2[0][:], a_rows[0][:].indirect(n2_l[:]))
+        for t in range(PACK):
+            diff = sb(f"diff{t}", [P, N], F32)
+            if t + 1 < PACK:
+                nc.vector.tensor_copy(at2[t + 1][:], a_rows[t + 1][:].indirect(n2_l[:]))
+            nc.vector.tensor_tensor(diff[:], a_rows[t][:].indirect(n1_l[:]), at2[t][:], ALU.subtract)
+            nc.scalar.activation(a_gained[:, t, :].rearrange("p (u m) -> p u m", u=PACK),
+                                 a_banks[t][:].rearrange("p (m u) -> p u m", u=PACK),
+                                 ACT.Copy, scale=ga_signed[:, t : t + 1])
+            nc.scalar.activation(gate[:, t, :].rearrange("p (u m) -> p m u", u=PACK),
+                                 diff[:].rearrange("p (m u) -> p m u", u=PACK),
+                                 ACT.Sigmoid, scale=0.0625)
+
+        b_gather(0)
+        z_bf = sb("z_bf", [P, N, PACK], BF16)
+        zw = sb("zw", [P, N], U32)
+        zs = sb("zs", [P, N], U8)
+        nc.vector.tensor_tensor(
+            z_bf[:].rearrange("p (c i) t -> p c t i", i=4),
+            a_gained[:].rearrange("p t (c i) -> p c t i", i=4),
+            gate[:].rearrange("p t (c i) -> p c t i", i=4),
+            ALU.mult,
+        )
+        b_quantize(0)
+        nc.vector.quantize_mx(out=zw[:].bitcast(FP8X4), scales=zs[:], in_=z_bf[:].rearrange("p n t -> p (n t)"))
+        b_gather(1)
+        b_quantize(1)
+
+        s_rows = [sb(f"s_row{t}", [P, N], F32) for t in range(PACK)]
+        for h in range(2):
+            cols = slice(HALF * h, HALF * (h + 1))
+            for t in (0, 2, 1, 3):
+                bank = psum.tile([P, HALF], F32, name=f"s_bank{h}{t}", tag=f"bank{4 * h + t}")
+                rows = slice(P * t, P * (t + 1))
+                product(bank[:], zw[:, rows], zs[:, rows], z2w[:, cols], z2s[:, cols])
+                nc.scalar.activation(s_rows[t][:, cols], bank[:], ACT.Copy, scale=0.0625)
+
+        out_rows = out_0.rearrange("(p t) v -> p t v", t=PACK)
+        y_bf = sb("y_bf", [P, N, PACK], BF16)
+        pb = [sb(f"pb{t}", [P, HALF], F32) for t in range(PACK)]
+        both = [sb(f"both{t}", [P, HALF], F32) for t in range(PACK)]
+        less = [sb(f"less{t}", [P, HALF], F32) for t in range(PACK)]
+        y = [sb(f"y{t}", [P, N], F32) for t in range(PACK)]
+        for pair in ((0, 2), (1, 3)):
+            for t in pair:
+                nc.vector.tensor_copy(pb[t][:], s_rows[t][:].indirect(n6_l[:]))
+                nc.scalar.activation(less[t][:], pb[t][:], ACT.Copy, scale=-2.0)
+            for t in pair:
+                nc.vector.tensor_tensor(both[t][:], s_rows[t][:].indirect(n5_l[:]), pb[t][:], ALU.add)
+            for t in pair:
+                nc.vector.tensor_tensor(y[t][:].indirect(n5_l[:]), both[t][:], three_quarters[:], ALU.mult)
+            for t in pair:
+                nc.vector.tensor_tensor(y[t][:].indirect(n6_l[:]), both[t][:], less[t][:], ALU.add)
+                nc.sync.dma_start(out_rows[:, t, :], y[t][:])
+                if t < PACK - 1:
+                    nc.scalar.copy(y_bf[:, :, t], y[t][:])
+
+        yw = sb("yw", [P, N], U32)
+        ys = sb("ys", [P, N], U8)
+        halves = [slice(0, HALF), slice(HALF, N)]
+        for cols in halves:
+            nc.vector.tensor_copy(y_bf[:, cols, PACK - 1], y[PACK - 1][:, cols])
+        for cols in halves:
+            nc.vector.quantize_mx(out=yw[:, cols].bitcast(FP8X4), scales=ys[:, cols],
+                                  in_=y_bf[:, cols, :].rearrange("p n t -> p (n t)"))
+            nc.sync.dma_start(as_words(out_1)[:, cols], yw[:].bitcast(I32)[:, cols])
+        for q in range(4):
+            eng = nc.scalar if q % 2 == 0 else nc.sync
+            eng.dma_start(out_2[0].bitcast(I32)[4 * q : 4 * q + 4, :], ys[:].bitcast(I32)[32 * q : 32 * q + 4, :])

@@ -34,8 +34,8 @@ def tile_picked_ckqcmpminmxhaar_none_po_kernel(
         keep = ctx.enter_context(tc.tile_pool(name="keep", bufs=1))
         psum = ctx.enter_context(tc.psum_pool(name="psum", bufs=1))
 
-        def sb(name, shape, dtype):
-            return keep.tile(shape, dtype, name=name, align_bytes=64)
+        def sb(name, shape, dtype, tag=None):
+            return keep.tile(shape, dtype, name=name, tag=tag or name, align_bytes=64)
 
         def load_list(name, dram):
             tile = sb(name, list(dram.shape), U16)
@@ -50,41 +50,41 @@ def tile_picked_ckqcmpminmxhaar_none_po_kernel(
         xs_in = sb("xs_in", [P, T], U8)
         ws_in = sb("ws_in", [P, N], U8)
         ds_placed = sb("ds_placed", [P, N], U8)
-        nc.vector.memset(ds_in[:].bitcast(I32), 0)
-        nc.gpsimd.memset(xs_in[:].bitcast(I32), 0)
         nc.gpsimd.memset(ws_in[:].bitcast(I32), 0)
-        nc.gpsimd.memset(ds_placed[:].bitcast(I32), 0)
-        warm = sb("warm", [P, 1], F32)
+        nc.vector.memset(xs_in[:].bitcast(I32), 0)
+        nc.gpsimd.memset(ds_in[:].bitcast(I32), 0)
+        nc.vector.memset(ds_placed[:].bitcast(I32), 0)
+        sixteenth = sb("sixteenth", [P, 1], F32)
         warm_out = sb("warm_out", [P, 1], F32)
-        nc.gpsimd.memset(warm[:], 0.0)
-        nc.scalar.activation(warm_out[:], warm[:], ACT.Sigmoid)
+        nc.vector.memset(sixteenth[:], 0.0625)
         three_quarters = sb("three_quarters", [P, HALF], F32)
-        nc.gpsimd.memset(three_quarters[:], 0.75)
+        nc.vector.memset(three_quarters[:], 0.75)
+        nc.scalar.activation(warm_out[:], three_quarters[:, 0:1], ACT.Sigmoid)
 
-        offs_l = load_list("offs_l", offs)
-        k1_l = load_list("k1_l", k1)
+        two_l = load_list("two_l", two)
         xw_in = sb("xw_in", [P, T], U32)
         nc.sync.dma_start(xw_in[:].bitcast(I32), as_words(x_words))
-        nc.sync.dma_start(ds_in[:].bitcast(I32)[0:P:8, :], d_scales[0].bitcast(I32))
-        dw_in = sb("dw_in", [P, G], U32)
-        nc.sync.dma_start(dw_in[:].bitcast(I32), as_words(d_words))
         for q in range(4):
-            nc.scalar.dma_start(xs_in[:].bitcast(I32)[32 * q : 32 * q + 4, :],
-                                x_scales[0].bitcast(I32)[4 * q : 4 * q + 4, :])
-        two_l = load_list("two_l", two)
-        ga_in = sb("ga_in", [P, PACK], F32)
-        gb_in = sb("gb_in", [P, PACK], F32)
-        nc.sync.dma_start(gb_in[:], gb.rearrange("(p t) o -> p (t o)", t=PACK))
-        nc.sync.dma_start(ga_in[:], ga.rearrange("(p t) o -> p (t o)", t=PACK))
-        n2_l = load_list("n2_l", n2)
-        n1_l = load_list("n1_l", n1)
+            nc.sync.dma_start(xs_in[:].bitcast(I32)[32 * q : 32 * q + 4, :],
+                              x_scales[0].bitcast(I32)[4 * q : 4 * q + 4, :])
         ww_in = sb("ww_in", [P, N], U32)
         nc.sync.dma_start(ww_in[:].bitcast(I32), as_words(w1_words))
         for q in range(4):
-            nc.gpsimd.dma_start(ws_in[:].bitcast(I32)[32 * q : 32 * q + 4, :],
-                                w1_scales[0].bitcast(I32)[4 * q : 4 * q + 4, :])
+            nc.sync.dma_start(ws_in[:].bitcast(I32)[32 * q : 32 * q + 4, :],
+                              w1_scales[0].bitcast(I32)[4 * q : 4 * q + 4, :])
+        ga_in = sb("ga_in", [P, PACK], F32)
+        gb_in = sb("gb_in", [P, PACK], F32)
+        nc.gpsimd.dma_start(gb_in[:], gb.rearrange("(p t) o -> p (t o)", t=PACK))
+        nc.gpsimd.dma_start(ga_in[:], ga.rearrange("(p t) o -> p (t o)", t=PACK))
+        k1_l = load_list("k1_l", k1)
+        nc.sync.dma_start(ds_in[:].bitcast(I32)[0:P:8, :], d_scales[0].bitcast(I32))
+        offs_l = load_list("offs_l", offs)
+        dw_in = sb("dw_in", [P, G], U32)
+        nc.sync.dma_start(dw_in[:].bitcast(I32), as_words(d_words))
         n3_l = load_list("n3_l", n3)
+        n2_l = load_list("n2_l", n2)
         n4_l = load_list("n4_l", n4)
+        n1_l = load_list("n1_l", n1)
         n6_l = load_list("n6_l", n6)
         n5_l = load_list("n5_l", n5)
 
@@ -96,130 +96,142 @@ def tile_picked_ckqcmpminmxhaar_none_po_kernel(
         nc.gpsimd.tensor_scalar(twice_nonneg[:], gb_in[:], 0.0, 2.0, ALU.is_ge, ALU.mult)
         nc.gpsimd.tensor_scalar(sign[:], twice_nonneg[:], 1.0, -1.0, ALU.mult, ALU.add)
         nc.gpsimd.tensor_tensor(gb_abs[:], gb_in[:], sign[:], ALU.mult)
-        nc.gpsimd.tensor_scalar(sign16[:], twice_nonneg[:], 0.0625, -0.0625, ALU.mult, ALU.add)
-        nc.gpsimd.tensor_tensor(ga_signed[:], ga_in[:], sign16[:], ALU.mult)
 
         ww = sb("ww", [P, N], U32)
         ws = sb("ws", [P, N], U8)
-        nc.gpsimd.tensor_copy(ww[:].rearrange("p (t m) -> p t m", t=PACK), ww_in[:].rearrange("p (m t) -> p t m", t=PACK))
-        nc.gpsimd.tensor_copy(ws[:].rearrange("p (t m) -> p t m", t=PACK), ws_in[:].rearrange("p (m t) -> p t m", t=PACK))
 
-        x1w = sb("x1w", [P, N], U32)
-        nc.vector.tensor_copy(x1w[:], xw_in[:].indirect(offs_l[:]))
-        ds_got = sb("ds_got", [P, N], U8)
-        ds_dealt = sb("ds_dealt", [P, N], U8)
-        nc.vector.tensor_copy(ds_got[:], ds_in[:].indirect(k1_l[:]))
-        x1s = sb("x1s", [P, N], U8)
-        nc.vector.tensor_copy(ds_dealt[:].rearrange("p (t m) -> p m t", t=PACK), ds_got[:].rearrange("p (m t) -> p m t", t=PACK))
-        for q in range(4):
-            nc.scalar.dma_start(ds_placed[:].bitcast(I32)[32 * q : 32 * q + 4, :],
-                                ds_dealt[:].bitcast(I32)[32 * q : 32 * q + 32 : 8, :])
-        dw_got = sb("dw_got", [P, N], U32)
-        nc.vector.tensor_copy(dw_got[:], dw_in[:].indirect(k1_l[:]))
-        nc.vector.tensor_copy(x1s[:], xs_in[:].indirect(offs_l[:]))
-        dw = sb("dw", [P, N], U32)
-        nc.vector.tensor_copy(dw[:].rearrange("p (t m) -> p m t", t=PACK), dw_got[:].rearrange("p (m t) -> p m t", t=PACK))
+        nc.gpsimd.tensor_scalar(sign16[:], twice_nonneg[:], 0.0625, -0.0625, ALU.mult, ALU.add)
+        nc.gpsimd.tensor_tensor(ga_signed[:], ga_in[:], sign16[:], ALU.mult)
+
         x2w = sb("x2w", [P, N], U32)
         nc.vector.tensor_copy(x2w[:], xw_in[:].indirect(two_l[:]))
         x2s = sb("x2s", [P, N], U8)
         nc.vector.tensor_copy(x2s[:], xs_in[:].indirect(two_l[:]))
+        nc.vector.tensor_copy(ww[:].rearrange("p (t m) -> p m t", t=PACK), ww_in[:].rearrange("p (m t) -> p m t", t=PACK))
+        nc.vector.tensor_copy(ws[:].rearrange("p (t m) -> p m t", t=PACK), ws_in[:].rearrange("p (m t) -> p m t", t=PACK))
+        ds_got = sb("ds_got", [P, N], U8)
+        ds_dealt = sb("ds_dealt", [P, N], U8)
+        nc.vector.tensor_copy(ds_got[:], ds_in[:].indirect(k1_l[:]))
+        dw_got = sb("dw_got", [P, N], U32)
+        nc.vector.tensor_copy(ds_dealt[:].rearrange("p (t m) -> p m t", t=PACK), ds_got[:].rearrange("p (m t) -> p m t", t=PACK))
+        for q in range(4):
+            nc.sync.dma_start(ds_placed[:].bitcast(I32)[32 * q : 32 * q + 4, :],
+                              ds_dealt[:].bitcast(I32)[32 * q : 32 * q + 32 : 8, :])
+        x1w = sb("x1w", [P, N], U32)
+        nc.vector.tensor_copy(x1w[:], xw_in[:].indirect(offs_l[:]))
+        nc.vector.tensor_copy(dw_got[:], dw_in[:].indirect(k1_l[:]))
+        x1s = sb("x1s", [P, N], U8)
+        nc.vector.tensor_copy(x1s[:], xs_in[:].indirect(offs_l[:]))
+        dw = sb("dw", [P, N], U32)
+        nc.vector.tensor_copy(dw[:].rearrange("p (t m) -> p m t", t=PACK), dw_got[:].rearrange("p (m t) -> p m t", t=PACK))
+
+        b_rows = []
+        b_all = sb("b_all", [P, PACK, N], F32)
+        for t in range(PACK):
+            bank = psum.tile([P, N], F32, name=f"b_bank{t}", tag=f"bank{t}")
+            cols = slice(P * t, P * (t + 1))
+            product(bank[:], ww[:, cols], ws[:, cols], x2w[:], x2s[:])
+            row = sb(f"b_row{t}", [P, 2 * N], F32)
+            nc.scalar.activation(row[:, 0:N], bank[:], ACT.Copy, scale=gb_abs[:, t : t + 1])
+            nc.scalar.activation(b_all[:, t, :], bank[:], ACT.Copy, scale=gb_abs[:, t : t + 1])
+            b_rows.append(row)
 
         a_rows = []
         a_gained = sb("a_gained", [P, PACK, N], F32)
         a_banks = []
         for t in range(PACK):
-            bank = psum.tile([P, N], F32, name=f"a_bank{t}", tag=f"bank{4 + t}")
+            bank = psum.tile([P, N], F32, name=f"a_bank{t}", tag=f"bank{t}")
             cols = slice(P * t, P * (t + 1))
             product(bank[:], dw[:, cols], ds_placed[:, cols], x1w[:], x1s[:])
             row = sb(f"a_row{t}", [P, 2 * N], F32)
-            nc.scalar.copy(row[:, 0:N], bank[:])
+            nc.scalar.activation(row[:, 0:N], bank[:], ACT.Copy, scale=sixteenth[:])
             a_rows.append(row)
             a_banks.append(bank)
 
-        b_rows = []
+        above = sb("above", [P, PACK, N], F32)
+        rise = sb("rise", [P, PACK, N], F32, tag="sixteenth")
+        larger = sb("larger", [P, PACK, N], F32)
         for t in range(PACK):
-            bank = psum.tile([P, N], F32, name=f"b_bank{t}", tag=f"bank{t}")
-            cols = slice(P * t, P * (t + 1))
-            product(bank[:], ww[:, cols], ws[:, cols], x2w[:], x2s[:])
-            row = sb(f"b_row{t}", [P, N], F32)
-            nc.scalar.activation(row[:], bank[:], ACT.Copy, scale=gb_abs[:, t : t + 1])
-            b_rows.append(row)
+            nc.vector.tensor_tensor(above[:, t, :], b_rows[t][:].indirect(n3_l[:]), b_all[:, t, :], ALU.subtract)
+        for t in range(PACK):
+            nc.scalar.activation(rise[:, t, :], above[:, t, :], ACT.Relu)
+        nc.gpsimd.tensor_tensor(larger[:], b_all[:], rise[:], ALU.add)
 
-        z2_bf = sb("z2_bf", [P, N, PACK], BF16)
-        z2w = sb("z2w", [P, N], U32)
-        z2s = sb("z2s", [P, N], U8)
-
-        def b_gather(h):
-            lists = slice(16 * h, 16 * (h + 1))
-            cols = slice(HALF * h, HALF * (h + 1))
-            at3 = sb(f"at3_{h}", [P, PACK, HALF], F32)
-            at4 = sb(f"at4_{h}", [P, PACK, HALF], F32)
-            larger = sb(f"larger{h}", [P, PACK, HALF], F32)
-            for t in range(PACK + 1):
-                if t < PACK:
-                    nc.vector.tensor_copy(at3[:, t, :], b_rows[t][:].indirect(n3_l[:, lists]))
-                if t > 0:
-                    nc.vector.tensor_copy(at4[:, t - 1, :], b_rows[t - 1][:].indirect(n4_l[:, lists]))
-                if t < PACK:
-                    nc.vector.tensor_tensor(larger[:, t, :], at3[:, t, :], b_rows[t][:, cols], ALU.max)
-            nc.vector.tensor_tensor(
-                z2_bf[:, cols, :].rearrange("p (c i) t -> p c t i", i=4),
-                larger[:].rearrange("p t (c i) -> p c t i", i=4),
-                at4[:].rearrange("p t (c i) -> p c t i", i=4),
-                ALU.min,
-            )
-
-        def b_quantize(h):
-            cols = slice(HALF * h, HALF * (h + 1))
-            nc.vector.quantize_mx(out=z2w[:, cols].bitcast(FP8X4), scales=z2s[:, cols],
-                                  in_=z2_bf[:, cols, :].rearrange("p n t -> p (n t)"))
+        at4_first = sb("at4_first", [P, PACK, HALF], F32, tag="x1w")
+        at2 = [sb(f"at2_{t}", [P, N], F32)[:] for t in range(PACK - 1)]
+        at2.append(at4_first[:, 2:4, :].rearrange("p t n -> p (t n)"))
+        for t in range(PACK):
+            nc.vector.tensor_copy(at2[t], a_rows[t][:].indirect(n2_l[:]))
+        for t in range(2):
+            nc.vector.tensor_copy(at4_first[:, t, :], b_rows[t][:].indirect(n4_l[:, 0:16]))
 
         gate = sb("gate", [P, PACK, N], F32)
-        at2 = [sb(f"at2_{t}", [P, N], F32) for t in range(PACK)]
-        nc.vector.tensor_copy(at2[0][:], a_rows[0][:].indirect(n2_l[:]))
         for t in range(PACK):
             diff = sb(f"diff{t}", [P, N], F32)
-            if t + 1 < PACK:
-                nc.vector.tensor_copy(at2[t + 1][:], a_rows[t + 1][:].indirect(n2_l[:]))
-            nc.vector.tensor_tensor(diff[:], a_rows[t][:].indirect(n1_l[:]), at2[t][:], ALU.subtract)
-            nc.scalar.activation(a_gained[:, t, :].rearrange("p (u m) -> p u m", u=PACK),
-                                 a_banks[t][:].rearrange("p (m u) -> p u m", u=PACK),
+            nc.vector.tensor_tensor(diff[:], a_rows[t][:].indirect(n1_l[:]), at2[t], ALU.subtract)
+            nc.scalar.activation(a_gained[:, t, :].rearrange("p (b a m) -> p b a m", a=2, b=2),
+                                 a_banks[t][:].rearrange("p (m a b) -> p b a m", a=2, b=2),
                                  ACT.Copy, scale=ga_signed[:, t : t + 1])
-            nc.scalar.activation(gate[:, t, :].rearrange("p (u m) -> p m u", u=PACK),
-                                 diff[:].rearrange("p (m u) -> p m u", u=PACK),
-                                 ACT.Sigmoid, scale=0.0625)
+            nc.scalar.activation(gate[:, t, :].rearrange("p (b a m) -> p m a b", a=2, b=2),
+                                 diff[:].rearrange("p (m a b) -> p m a b", a=2, b=2),
+                                 ACT.Sigmoid)
 
-        b_gather(0)
-        z_bf = sb("z_bf", [P, N, PACK], BF16)
-        zw = sb("zw", [P, N], U32)
-        zs = sb("zs", [P, N], U8)
-        nc.vector.tensor_tensor(
-            z_bf[:].rearrange("p (c i) t -> p c t i", i=4),
-            a_gained[:].rearrange("p t (c i) -> p c t i", i=4),
-            gate[:].rearrange("p t (c i) -> p c t i", i=4),
-            ALU.mult,
-        )
-        b_quantize(0)
-        nc.vector.quantize_mx(out=zw[:].bitcast(FP8X4), scales=zs[:], in_=z_bf[:].rearrange("p n t -> p (n t)"))
-        b_gather(1)
-        b_quantize(1)
+        at4_second = sb("at4_second", [P, PACK, HALF], F32, tag="a_row3")
+        for t in range(2, PACK):
+            nc.vector.tensor_copy(at4_first[:, t, :], b_rows[t][:].indirect(n4_l[:, 0:16]))
+        for t in range(PACK):
+            nc.vector.tensor_copy(at4_second[:, t, :], b_rows[t][:].indirect(n4_l[:, 16:32]))
+        at4 = [at4_first, at4_second]
 
+        z2_bf = [sb(f"z2_bf{h}", [P, HALF, PACK], BF16) for h in range(2)]
+        z2w = sb("z2w", [P, N], U32)
+        z2s = sb("z2s", [P, N], U8)
+        zw = [sb(f"zw{h}", [P, HALF], U32) for h in range(2)]
+        zs = [sb(f"zs{h}", [P, HALF], U8) for h in range(2)]
+
+        def interleaved(engine, out, in0, in1, op):
+            engine.tensor_tensor(out.rearrange("p (c i) t -> p c t i", i=4),
+                                 in0.rearrange("p t (c i) -> p c t i", i=4),
+                                 in1.rearrange("p t (c i) -> p c t i", i=4), op)
+
+        def quantize(words, scales, values):
+            nc.vector.quantize_mx(out=words.bitcast(FP8X4), scales=scales, in_=values.rearrange("p n t -> p (n t)"))
+
+        halves = [slice(0, HALF), slice(HALF, N)]
         s_rows = [sb(f"s_row{t}", [P, N], F32) for t in range(PACK)]
+
+        def s_product(t, cols, tag):
+            bank = psum.tile([P, cols.stop - cols.start], F32, name=f"s_{tag}", tag=tag)
+            rows = slice(P * (t // 2), P * (t // 2 + 1))
+            product(bank[:], zw[t % 2][:, rows], zs[t % 2][:, rows], z2w[:, cols], z2s[:, cols])
+            nc.scalar.activation(s_rows[t][:, cols], bank[:], ACT.Copy, scale=0.0625)
+
+        z_even = sb("z_even", [P, HALF, PACK], BF16)
+        z_planes = sb("z_planes", [P, PACK, HALF], BF16)
+        nc.gpsimd.tensor_tensor(z_planes[:], a_gained[:, :, halves[0]], gate[:, :, halves[0]], ALU.mult)
+        nc.scalar.copy(z_even[:].rearrange("p (c i) t -> p c t i", i=4), z_planes[:].rearrange("p t (c i) -> p c t i", i=4))
         for h in range(2):
-            cols = slice(HALF * h, HALF * (h + 1))
-            for t in (0, 2, 1, 3):
-                bank = psum.tile([P, HALF], F32, name=f"s_bank{h}{t}", tag=f"bank{4 * h + t}")
-                rows = slice(P * t, P * (t + 1))
-                product(bank[:], zw[:, rows], zs[:, rows], z2w[:, cols], z2s[:, cols])
-                nc.scalar.activation(s_rows[t][:, cols], bank[:], ACT.Copy, scale=0.0625)
+            interleaved(nc.vector, z2_bf[h][:], larger[:, :, halves[h]], at4[h][:], ALU.min)
+        quantize(z2w[:, halves[0]], z2s[:, halves[0]], z2_bf[0][:])
+        quantize(zw[0][:], zs[0][:], z_even[:])
+        quantize(z2w[:, halves[1]], z2s[:, halves[1]], z2_bf[1][:])
+        for t in (0, 2):
+            for h in range(2):
+                s_product(t, halves[h], f"bank{4 + t + h}")
+        z_odd = sb("z_odd", [P, HALF, PACK], BF16, tag="z_even")
+        interleaved(nc.vector, z_odd[:], a_gained[:, :, halves[1]], gate[:, :, halves[1]], ALU.mult)
+        quantize(zw[1][:], zs[1][:], z_odd[:])
+        for t in (3, 1):
+            s_product(t, slice(0, N), f"bank{t}")
 
         out_rows = out_0.rearrange("(p t) v -> p t v", t=PACK)
         y_bf = sb("y_bf", [P, N, PACK], BF16)
-        pb = [sb(f"pb{t}", [P, HALF], F32) for t in range(PACK)]
-        both = [sb(f"both{t}", [P, HALF], F32) for t in range(PACK)]
-        less = [sb(f"less{t}", [P, HALF], F32) for t in range(PACK)]
         y = [sb(f"y{t}", [P, N], F32) for t in range(PACK)]
-        for pair in ((0, 2), (1, 3)):
+        reuse = {3: "both0", 1: "less0"}
+        for pair in ((0, 2), (3, 1)):
+            pb = {t: sb(f"pb{t}", [P, HALF], F32, tag=reuse.get(t)) for t in pair}
+            both = {t: sb(f"both{t}", [P, HALF], F32) for t in pair}
+            less = {t: sb(f"less{t}", [P, HALF], F32) for t in pair}
             for t in pair:
                 nc.vector.tensor_copy(pb[t][:], s_rows[t][:].indirect(n6_l[:]))
                 nc.scalar.activation(less[t][:], pb[t][:], ACT.Copy, scale=-2.0)
@@ -230,14 +242,13 @@ def tile_picked_ckqcmpminmxhaar_none_po_kernel(
             for t in pair:
                 nc.vector.tensor_tensor(y[t][:].indirect(n6_l[:]), both[t][:], less[t][:], ALU.add)
                 nc.sync.dma_start(out_rows[:, t, :], y[t][:])
-                if t < PACK - 1:
+                if t != 1:
                     nc.scalar.copy(y_bf[:, :, t], y[t][:])
 
         yw = sb("yw", [P, N], U32)
         ys = sb("ys", [P, N], U8)
-        halves = [slice(0, HALF), slice(HALF, N)]
         for cols in halves:
-            nc.vector.tensor_copy(y_bf[:, cols, PACK - 1], y[PACK - 1][:, cols])
+            nc.vector.tensor_copy(y_bf[:, cols, 1], y[1][:, cols])
         for cols in halves:
             nc.vector.quantize_mx(out=yw[:, cols].bitcast(FP8X4), scales=ys[:, cols],
                                   in_=y_bf[:, cols, :].rearrange("p n t -> p (n t)"))

@@ -15,10 +15,15 @@ ACT = mybir.ActivationFunctionType
 P = 128
 PACK = 4
 N = 512
-HALF = 256
+HALF = N // 2
 T = 1024
 G = 2048
-FLOPS = 3 * 2 * 512 * 512 * 512
+QUADS = 4
+GROUP = 16
+RUN = 4
+RELU_PLANES = 2
+LAST = 1
+FLOPS = 3 * 2 * N * N * N
 
 
 def as_words(dram):
@@ -42,9 +47,39 @@ def tile_picked_ckqcmpminmxhaar_none_po_kernel(
             nc.sync.dma_start(tile[:], dram)
             return tile
 
-        def product(bank, lw, ls, rw, rs):
-            nc.tensor.matmul_mx(out=bank, lhsT=lw.bitcast(FP8X4), lhsT_scale=ls,
-                                rhs=rw.bitcast(FP8X4), rhs_scale=rs, start=True, stop=True)
+        def load_words(name, dram, columns):
+            tile = sb(name, [P, columns], U32)
+            nc.sync.dma_start(tile[:].bitcast(I32), as_words(dram))
+            return tile
+
+        def load_scales(tile, dram):
+            for q in range(QUADS):
+                nc.sync.dma_start(tile[:].bitcast(I32)[32 * q : 32 * q + 4, :],
+                                  dram[0].bitcast(I32)[4 * q : 4 * q + 4, :])
+
+        def gather(name, window, offsets, dtype):
+            tile = sb(name, [P, N], dtype)
+            nc.vector.tensor_copy(tile[:], window[:].indirect(offsets[:]))
+            return tile
+
+        def deal(name, source, dtype):
+            tile = sb(name, [P, N], dtype)
+            nc.vector.tensor_copy(tile[:].rearrange("p (t m) -> p m t", t=PACK),
+                                  source[:].rearrange("p (m t) -> p m t", t=PACK))
+            return tile
+
+        def product(bank, lhs_words, lhs_scales, rhs_words, rhs_scales):
+            nc.tensor.matmul_mx(out=bank, lhsT=lhs_words.bitcast(FP8X4), lhsT_scale=lhs_scales,
+                                rhs=rhs_words.bitcast(FP8X4), rhs_scale=rhs_scales, start=True, stop=True)
+
+        def word_side(values):
+            return values.rearrange("p (c i) t -> p c t i", i=RUN)
+
+        def plane_side(values):
+            return values.rearrange("p t (c i) -> p c t i", i=RUN)
+
+        def quantize(words, scales, values):
+            nc.vector.quantize_mx(out=words.bitcast(FP8X4), scales=scales, in_=values.rearrange("p n t -> p (n t)"))
 
         ds_in = sb("ds_in", [P, G], U8)
         xs_in = sb("xs_in", [P, T], U8)
@@ -54,24 +89,14 @@ def tile_picked_ckqcmpminmxhaar_none_po_kernel(
         nc.vector.memset(xs_in[:].bitcast(I32), 0)
         nc.gpsimd.memset(ds_in[:].bitcast(I32), 0)
         nc.vector.memset(ds_placed[:].bitcast(I32), 0)
-        sixteenth = sb("sixteenth", [P, 1], F32)
-        warm_out = sb("warm_out", [P, 1], F32)
-        nc.vector.memset(sixteenth[:], 0.0625)
         three_quarters = sb("three_quarters", [P, HALF], F32)
         nc.vector.memset(three_quarters[:], 0.75)
-        nc.scalar.activation(warm_out[:], three_quarters[:, 0:1], ACT.Sigmoid)
 
         two_l = load_list("two_l", two)
-        xw_in = sb("xw_in", [P, T], U32)
-        nc.sync.dma_start(xw_in[:].bitcast(I32), as_words(x_words))
-        for q in range(4):
-            nc.sync.dma_start(xs_in[:].bitcast(I32)[32 * q : 32 * q + 4, :],
-                              x_scales[0].bitcast(I32)[4 * q : 4 * q + 4, :])
-        ww_in = sb("ww_in", [P, N], U32)
-        nc.sync.dma_start(ww_in[:].bitcast(I32), as_words(w1_words))
-        for q in range(4):
-            nc.sync.dma_start(ws_in[:].bitcast(I32)[32 * q : 32 * q + 4, :],
-                              w1_scales[0].bitcast(I32)[4 * q : 4 * q + 4, :])
+        xw_in = load_words("xw_in", x_words, T)
+        load_scales(xs_in, x_scales)
+        ww_in = load_words("ww_in", w1_words, N)
+        load_scales(ws_in, w1_scales)
         ga_in = sb("ga_in", [P, PACK], F32)
         gb_in = sb("gb_in", [P, PACK], F32)
         nc.gpsimd.dma_start(gb_in[:], gb.rearrange("(p t) o -> p (t o)", t=PACK))
@@ -79,8 +104,7 @@ def tile_picked_ckqcmpminmxhaar_none_po_kernel(
         k1_l = load_list("k1_l", k1)
         nc.sync.dma_start(ds_in[:].bitcast(I32)[0:P:8, :], d_scales[0].bitcast(I32))
         offs_l = load_list("offs_l", offs)
-        dw_in = sb("dw_in", [P, G], U32)
-        nc.sync.dma_start(dw_in[:].bitcast(I32), as_words(d_words))
+        dw_in = load_words("dw_in", d_words, G)
         n3_l = load_list("n3_l", n3)
         n2_l = load_list("n2_l", n2)
         n4_l = load_list("n4_l", n4)
@@ -90,136 +114,116 @@ def tile_picked_ckqcmpminmxhaar_none_po_kernel(
 
         twice_nonneg = sb("twice_nonneg", [P, PACK], F32)
         sign = sb("sign", [P, PACK], F32)
-        sign16 = sb("sign16", [P, PACK], F32)
+        sign_16th = sb("sign_16th", [P, PACK], F32)
         gb_abs = sb("gb_abs", [P, PACK], F32)
         ga_signed = sb("ga_signed", [P, PACK], F32)
         nc.gpsimd.tensor_scalar(twice_nonneg[:], gb_in[:], 0.0, 2.0, ALU.is_ge, ALU.mult)
         nc.gpsimd.tensor_scalar(sign[:], twice_nonneg[:], 1.0, -1.0, ALU.mult, ALU.add)
         nc.gpsimd.tensor_tensor(gb_abs[:], gb_in[:], sign[:], ALU.mult)
+        nc.gpsimd.tensor_scalar(sign_16th[:], twice_nonneg[:], 0.0625, -0.0625, ALU.mult, ALU.add)
+        nc.gpsimd.tensor_tensor(ga_signed[:], ga_in[:], sign_16th[:], ALU.mult)
 
-        ww = sb("ww", [P, N], U32)
-        ws = sb("ws", [P, N], U8)
-
-        nc.gpsimd.tensor_scalar(sign16[:], twice_nonneg[:], 0.0625, -0.0625, ALU.mult, ALU.add)
-        nc.gpsimd.tensor_tensor(ga_signed[:], ga_in[:], sign16[:], ALU.mult)
-
-        x2w = sb("x2w", [P, N], U32)
-        nc.vector.tensor_copy(x2w[:], xw_in[:].indirect(two_l[:]))
-        x2s = sb("x2s", [P, N], U8)
-        nc.vector.tensor_copy(x2s[:], xs_in[:].indirect(two_l[:]))
-        nc.vector.tensor_copy(ww[:].rearrange("p (t m) -> p m t", t=PACK), ww_in[:].rearrange("p (m t) -> p m t", t=PACK))
-        nc.vector.tensor_copy(ws[:].rearrange("p (t m) -> p m t", t=PACK), ws_in[:].rearrange("p (m t) -> p m t", t=PACK))
-        ds_got = sb("ds_got", [P, N], U8)
-        ds_dealt = sb("ds_dealt", [P, N], U8)
-        nc.vector.tensor_copy(ds_got[:], ds_in[:].indirect(k1_l[:]))
-        dw_got = sb("dw_got", [P, N], U32)
-        nc.vector.tensor_copy(ds_dealt[:].rearrange("p (t m) -> p m t", t=PACK), ds_got[:].rearrange("p (m t) -> p m t", t=PACK))
-        for q in range(4):
+        x2w = gather("x2w", xw_in, two_l, U32)
+        x2s = gather("x2s", xs_in, two_l, U8)
+        ww = deal("ww", ww_in, U32)
+        ws = deal("ws", ws_in, U8)
+        ds_got = gather("ds_got", ds_in, k1_l, U8)
+        ds_dealt = deal("ds_dealt", ds_got, U8)
+        for q in range(QUADS):
             nc.sync.dma_start(ds_placed[:].bitcast(I32)[32 * q : 32 * q + 4, :],
                               ds_dealt[:].bitcast(I32)[32 * q : 32 * q + 32 : 8, :])
-        x1w = sb("x1w", [P, N], U32)
-        nc.vector.tensor_copy(x1w[:], xw_in[:].indirect(offs_l[:]))
-        nc.vector.tensor_copy(dw_got[:], dw_in[:].indirect(k1_l[:]))
-        x1s = sb("x1s", [P, N], U8)
-        nc.vector.tensor_copy(x1s[:], xs_in[:].indirect(offs_l[:]))
-        dw = sb("dw", [P, N], U32)
-        nc.vector.tensor_copy(dw[:].rearrange("p (t m) -> p m t", t=PACK), dw_got[:].rearrange("p (m t) -> p m t", t=PACK))
+        x1w = gather("x1w", xw_in, offs_l, U32)
+        dw_got = gather("dw_got", dw_in, k1_l, U32)
+        x1s = gather("x1s", xs_in, offs_l, U8)
+        dw = deal("dw", dw_got, U32)
 
         b_rows = []
-        b_all = sb("b_all", [P, PACK, N], F32)
+        b_banks = []
+        b_copy = sb("b_copy", [P, RELU_PLANES, N], F32)
         for t in range(PACK):
             bank = psum.tile([P, N], F32, name=f"b_bank{t}", tag=f"bank{t}")
             cols = slice(P * t, P * (t + 1))
             product(bank[:], ww[:, cols], ws[:, cols], x2w[:], x2s[:])
             row = sb(f"b_row{t}", [P, 2 * N], F32)
             nc.scalar.activation(row[:, 0:N], bank[:], ACT.Copy, scale=gb_abs[:, t : t + 1])
-            nc.scalar.activation(b_all[:, t, :], bank[:], ACT.Copy, scale=gb_abs[:, t : t + 1])
+            if t < RELU_PLANES:
+                nc.scalar.activation(b_copy[:, t, :], bank[:], ACT.Copy, scale=gb_abs[:, t : t + 1])
             b_rows.append(row)
+            b_banks.append(bank)
+
+        above = sb("above", [P, RELU_PLANES, N], F32)
+        rise = sb("rise", [P, RELU_PLANES, N], F32)
+        at3 = sb("at3", [P, PACK - RELU_PLANES, N], F32)
+        larger = sb("larger", [P, PACK, N], F32)
+        for t in range(RELU_PLANES):
+            nc.vector.tensor_tensor(above[:, t, :], b_rows[t][:].indirect(n3_l[:]), b_copy[:, t, :], ALU.subtract)
+        nc.scalar.activation(rise[:], above[:], ACT.Relu)
+        nc.gpsimd.tensor_tensor(larger[:, 0:RELU_PLANES, :], b_copy[:], rise[:], ALU.add)
+        for t in range(RELU_PLANES, PACK):
+            nc.vector.tensor_copy(at3[:, t - RELU_PLANES, :], b_rows[t][:].indirect(n3_l[:]))
+        for t in range(RELU_PLANES, PACK):
+            nc.vector.scalar_tensor_tensor(larger[:, t, :], b_banks[t][:], gb_abs[:, t : t + 1],
+                                           at3[:, t - RELU_PLANES, :], ALU.mult, ALU.max)
 
         a_rows = []
-        a_gained = sb("a_gained", [P, PACK, N], F32)
         a_banks = []
         for t in range(PACK):
-            bank = psum.tile([P, N], F32, name=f"a_bank{t}", tag=f"bank{t}")
+            bank = psum.tile([P, N], F32, name=f"a_bank{t}", tag=f"bank{t if t < RELU_PLANES else t + RELU_PLANES}")
             cols = slice(P * t, P * (t + 1))
             product(bank[:], dw[:, cols], ds_placed[:, cols], x1w[:], x1s[:])
             row = sb(f"a_row{t}", [P, 2 * N], F32)
-            nc.scalar.activation(row[:, 0:N], bank[:], ACT.Copy, scale=sixteenth[:])
+            nc.scalar.copy(row[:, 0:N], bank[:])
             a_rows.append(row)
             a_banks.append(bank)
 
-        above = sb("above", [P, PACK, N], F32)
-        rise = sb("rise", [P, PACK, N], F32, tag="sixteenth")
-        larger = sb("larger", [P, PACK, N], F32)
-        for t in range(PACK):
-            nc.vector.tensor_tensor(above[:, t, :], b_rows[t][:].indirect(n3_l[:]), b_all[:, t, :], ALU.subtract)
-        for t in range(PACK):
-            nc.scalar.activation(rise[:, t, :], above[:, t, :], ACT.Relu)
-        nc.gpsimd.tensor_tensor(larger[:], b_all[:], rise[:], ALU.add)
-
-        at4_first = sb("at4_first", [P, PACK, HALF], F32, tag="x1w")
-        at2 = [sb(f"at2_{t}", [P, N], F32)[:] for t in range(PACK - 1)]
-        at2.append(at4_first[:, 2:4, :].rearrange("p t n -> p (t n)"))
-        for t in range(PACK):
-            nc.vector.tensor_copy(at2[t], a_rows[t][:].indirect(n2_l[:]))
-        for t in range(2):
-            nc.vector.tensor_copy(at4_first[:, t, :], b_rows[t][:].indirect(n4_l[:, 0:16]))
-
+        at2 = [gather(f"at2_{t}", a_rows[t], n2_l, F32) for t in range(PACK)]
+        a_gained = sb("a_gained", [P, PACK, N], F32)
         gate = sb("gate", [P, PACK, N], F32)
         for t in range(PACK):
             diff = sb(f"diff{t}", [P, N], F32)
-            nc.vector.tensor_tensor(diff[:], a_rows[t][:].indirect(n1_l[:]), at2[t], ALU.subtract)
-            nc.scalar.activation(a_gained[:, t, :].rearrange("p (b a m) -> p b a m", a=2, b=2),
-                                 a_banks[t][:].rearrange("p (m a b) -> p b a m", a=2, b=2),
+            nc.vector.tensor_tensor(diff[:], a_rows[t][:].indirect(n1_l[:]), at2[t][:], ALU.subtract)
+            nc.scalar.activation(a_gained[:, t, :].rearrange("p (o e m) -> p o e m", e=2, o=2),
+                                 a_banks[t][:].rearrange("p (m e o) -> p o e m", e=2, o=2),
                                  ACT.Copy, scale=ga_signed[:, t : t + 1])
-            nc.scalar.activation(gate[:, t, :].rearrange("p (b a m) -> p m a b", a=2, b=2),
-                                 diff[:].rearrange("p (m a b) -> p m a b", a=2, b=2),
-                                 ACT.Sigmoid)
+            nc.scalar.activation(gate[:, t, :].rearrange("p (o e m) -> p m e o", e=2, o=2),
+                                 diff[:].rearrange("p (m e o) -> p m e o", e=2, o=2),
+                                 ACT.Sigmoid, scale=0.0625)
 
-        at4_second = sb("at4_second", [P, PACK, HALF], F32, tag="a_row3")
-        for t in range(2, PACK):
-            nc.vector.tensor_copy(at4_first[:, t, :], b_rows[t][:].indirect(n4_l[:, 0:16]))
-        for t in range(PACK):
-            nc.vector.tensor_copy(at4_second[:, t, :], b_rows[t][:].indirect(n4_l[:, 16:32]))
-        at4 = [at4_first, at4_second]
+        halves = [slice(0, HALF), slice(HALF, N)]
+        at4 = sb("at4", [P, 2, PACK, HALF], F32, tag=f"a_row{PACK - 1}")
+        for h, cols in enumerate(halves):
+            entries = slice(cols.start // GROUP, cols.stop // GROUP)
+            for t in range(PACK):
+                nc.vector.tensor_copy(at4[:, h, t, :], b_rows[t][:].indirect(n4_l[:, entries]))
 
         z2_bf = [sb(f"z2_bf{h}", [P, HALF, PACK], BF16) for h in range(2)]
         z2w = sb("z2w", [P, N], U32)
         z2s = sb("z2s", [P, N], U8)
-        zw = [sb(f"zw{h}", [P, HALF], U32) for h in range(2)]
-        zs = [sb(f"zs{h}", [P, HALF], U8) for h in range(2)]
-
-        def interleaved(engine, out, in0, in1, op):
-            engine.tensor_tensor(out.rearrange("p (c i) t -> p c t i", i=4),
-                                 in0.rearrange("p t (c i) -> p c t i", i=4),
-                                 in1.rearrange("p t (c i) -> p c t i", i=4), op)
-
-        def quantize(words, scales, values):
-            nc.vector.quantize_mx(out=words.bitcast(FP8X4), scales=scales, in_=values.rearrange("p n t -> p (n t)"))
-
-        halves = [slice(0, HALF), slice(HALF, N)]
+        zw = [sb(f"zw{odd}", [P, HALF], U32) for odd in range(2)]
+        zs = [sb(f"zs{odd}", [P, HALF], U8) for odd in range(2)]
         s_rows = [sb(f"s_row{t}", [P, N], F32) for t in range(PACK)]
 
         def s_product(t, cols, tag):
             bank = psum.tile([P, cols.stop - cols.start], F32, name=f"s_{tag}", tag=tag)
-            rows = slice(P * (t // 2), P * (t // 2 + 1))
-            product(bank[:], zw[t % 2][:, rows], zs[t % 2][:, rows], z2w[:, cols], z2s[:, cols])
+            places = slice(P * (t // 2), P * (t // 2 + 1))
+            product(bank[:], zw[t % 2][:, places], zs[t % 2][:, places], z2w[:, cols], z2s[:, cols])
             nc.scalar.activation(s_rows[t][:, cols], bank[:], ACT.Copy, scale=0.0625)
 
         z_even = sb("z_even", [P, HALF, PACK], BF16)
         z_planes = sb("z_planes", [P, PACK, HALF], BF16)
         nc.gpsimd.tensor_tensor(z_planes[:], a_gained[:, :, halves[0]], gate[:, :, halves[0]], ALU.mult)
-        nc.scalar.copy(z_even[:].rearrange("p (c i) t -> p c t i", i=4), z_planes[:].rearrange("p t (c i) -> p c t i", i=4))
-        for h in range(2):
-            interleaved(nc.vector, z2_bf[h][:], larger[:, :, halves[h]], at4[h][:], ALU.min)
+        nc.scalar.copy(word_side(z_even[:]), plane_side(z_planes[:]))
+        for h, cols in enumerate(halves):
+            nc.vector.tensor_tensor(word_side(z2_bf[h][:]), plane_side(larger[:, :, cols]), plane_side(at4[:, h]), ALU.min)
         quantize(z2w[:, halves[0]], z2s[:, halves[0]], z2_bf[0][:])
         quantize(zw[0][:], zs[0][:], z_even[:])
         quantize(z2w[:, halves[1]], z2s[:, halves[1]], z2_bf[1][:])
         for t in (0, 2):
-            for h in range(2):
-                s_product(t, halves[h], f"bank{4 + t + h}")
+            for h, cols in enumerate(halves):
+                s_product(t, cols, f"bank{PACK + t + h}")
         z_odd = sb("z_odd", [P, HALF, PACK], BF16, tag="z_even")
-        interleaved(nc.vector, z_odd[:], a_gained[:, :, halves[1]], gate[:, :, halves[1]], ALU.mult)
+        nc.vector.tensor_tensor(word_side(z_odd[:]), plane_side(a_gained[:, :, halves[1]]),
+                                plane_side(gate[:, :, halves[1]]), ALU.mult)
         quantize(zw[1][:], zs[1][:], z_odd[:])
         for t in (3, 1):
             s_product(t, slice(0, N), f"bank{t}")
@@ -227,32 +231,31 @@ def tile_picked_ckqcmpminmxhaar_none_po_kernel(
         out_rows = out_0.rearrange("(p t) v -> p t v", t=PACK)
         y_bf = sb("y_bf", [P, N, PACK], BF16)
         y = [sb(f"y{t}", [P, N], F32) for t in range(PACK)]
-        reuse = {3: "both0", 1: "less0"}
-        for pair in ((0, 2), (3, 1)):
+        reuse = {3: "both0", LAST: "minus_two_pb0"}
+        for pair in ((0, 2), (3, LAST)):
             pb = {t: sb(f"pb{t}", [P, HALF], F32, tag=reuse.get(t)) for t in pair}
             both = {t: sb(f"both{t}", [P, HALF], F32) for t in pair}
-            less = {t: sb(f"less{t}", [P, HALF], F32) for t in pair}
+            minus_two_pb = {t: sb(f"minus_two_pb{t}", [P, HALF], F32) for t in pair}
             for t in pair:
                 nc.vector.tensor_copy(pb[t][:], s_rows[t][:].indirect(n6_l[:]))
-                nc.scalar.activation(less[t][:], pb[t][:], ACT.Copy, scale=-2.0)
+                nc.scalar.activation(minus_two_pb[t][:], pb[t][:], ACT.Copy, scale=-2.0)
             for t in pair:
                 nc.vector.tensor_tensor(both[t][:], s_rows[t][:].indirect(n5_l[:]), pb[t][:], ALU.add)
             for t in pair:
                 nc.vector.tensor_tensor(y[t][:].indirect(n5_l[:]), both[t][:], three_quarters[:], ALU.mult)
             for t in pair:
-                nc.vector.tensor_tensor(y[t][:].indirect(n6_l[:]), both[t][:], less[t][:], ALU.add)
+                nc.vector.tensor_tensor(y[t][:].indirect(n6_l[:]), both[t][:], minus_two_pb[t][:], ALU.add)
                 nc.sync.dma_start(out_rows[:, t, :], y[t][:])
-                if t != 1:
+                if t != LAST:
                     nc.scalar.copy(y_bf[:, :, t], y[t][:])
 
         yw = sb("yw", [P, N], U32)
         ys = sb("ys", [P, N], U8)
         for cols in halves:
-            nc.vector.tensor_copy(y_bf[:, cols, 1], y[1][:, cols])
+            nc.vector.tensor_copy(y_bf[:, cols, LAST], y[LAST][:, cols])
         for cols in halves:
-            nc.vector.quantize_mx(out=yw[:, cols].bitcast(FP8X4), scales=ys[:, cols],
-                                  in_=y_bf[:, cols, :].rearrange("p n t -> p (n t)"))
+            quantize(yw[:, cols], ys[:, cols], y_bf[:, cols, :])
             nc.sync.dma_start(as_words(out_1)[:, cols], yw[:].bitcast(I32)[:, cols])
-        for q in range(4):
-            eng = nc.scalar if q % 2 == 0 else nc.sync
-            eng.dma_start(out_2[0].bitcast(I32)[4 * q : 4 * q + 4, :], ys[:].bitcast(I32)[32 * q : 32 * q + 4, :])
+        for q in range(QUADS):
+            queue = nc.scalar if q % 2 == 0 else nc.sync
+            queue.dma_start(out_2[0].bitcast(I32)[4 * q : 4 * q + 4, :], ys[:].bitcast(I32)[32 * q : 32 * q + 4, :])

from contextlib import ExitStack

import concourse.mybir as mybir

F32 = mybir.dt.float32
BF16 = mybir.dt.bfloat16
I32 = mybir.dt.int32
U32 = mybir.dt.uint32
U16 = mybir.dt.uint16
U8 = mybir.dt.uint8
FP8X4 = mybir.dt.float8_e4m3fn_x4
ALU = mybir.AluOpType
ACT = mybir.ActivationFunctionType

P = 128
PACK = 4
N = 512
HALF = N // 2
T = 1024
G = 2048
QUADS = 4
GROUP = 16
RUN = 4
RELU_PLANES = 2
LAST = 1
FLOPS = 3 * 2 * N * N * N


def as_words(dram):
    return dram[0].rearrange("p n t -> p (n t)").bitcast(I32)


def tile_picked_ckqcmpminmxhaar_none_po_kernel(
    tc, x_words, x_scales, d_words, d_scales, w1_words, w1_scales, ga, gb,
    offs, k1, two, n1, n2, n3, n4, n5, n6, out_0, out_1, out_2,
):
    nc = tc.nc
    with ExitStack() as ctx:
        keep = ctx.enter_context(tc.tile_pool(name="keep", bufs=1))
        psum = ctx.enter_context(tc.psum_pool(name="psum", bufs=1))

        def sb(name, shape, dtype, tag=None):
            return keep.tile(shape, dtype, name=name, tag=tag or name, align_bytes=64)

        def load_list(name, dram):
            tile = sb(name, list(dram.shape), U16)
            nc.sync.dma_start(tile[:], dram)
            return tile

        def load_words(name, dram, columns):
            tile = sb(name, [P, columns], U32)
            nc.sync.dma_start(tile[:].bitcast(I32), as_words(dram))
            return tile

        def load_scales(tile, dram):
            for q in range(QUADS):
                nc.sync.dma_start(tile[:].bitcast(I32)[32 * q : 32 * q + 4, :],
                                  dram[0].bitcast(I32)[4 * q : 4 * q + 4, :])

        def gather(name, window, offsets, dtype):
            tile = sb(name, [P, N], dtype)
            nc.vector.tensor_copy(tile[:], window[:].indirect(offsets[:]))
            return tile

        def deal(name, source, dtype):
            tile = sb(name, [P, N], dtype)
            nc.vector.tensor_copy(tile[:].rearrange("p (t m) -> p m t", t=PACK),
                                  source[:].rearrange("p (m t) -> p m t", t=PACK))
            return tile

        def product(bank, lhs_words, lhs_scales, rhs_words, rhs_scales):
            nc.tensor.matmul_mx(out=bank, lhsT=lhs_words.bitcast(FP8X4), lhsT_scale=lhs_scales,
                                rhs=rhs_words.bitcast(FP8X4), rhs_scale=rhs_scales, start=True, stop=True)

        def word_side(values):
            return values.rearrange("p (c i) t -> p c t i", i=RUN)

        def plane_side(values):
            return values.rearrange("p t (c i) -> p c t i", i=RUN)

        def quantize(words, scales, values):
            nc.vector.quantize_mx(out=words.bitcast(FP8X4), scales=scales, in_=values.rearrange("p n t -> p (n t)"))

        ds_in = sb("ds_in", [P, G], U8)
        xs_in = sb("xs_in", [P, T], U8)
        ws_in = sb("ws_in", [P, N], U8)
        ds_placed = sb("ds_placed", [P, N], U8)
        nc.gpsimd.memset(ws_in[:].bitcast(I32), 0)
        nc.vector.memset(xs_in[:].bitcast(I32), 0)
        nc.gpsimd.memset(ds_in[:].bitcast(I32), 0)
        nc.vector.memset(ds_placed[:].bitcast(I32), 0)
        three_quarters = sb("three_quarters", [P, HALF], F32)
        nc.vector.memset(three_quarters[:], 0.75)

        two_l = load_list("two_l", two)
        xw_in = load_words("xw_in", x_words, T)
        load_scales(xs_in, x_scales)
        ww_in = load_words("ww_in", w1_words, N)
        load_scales(ws_in, w1_scales)
        ga_in = sb("ga_in", [P, PACK], F32)
        gb_in = sb("gb_in", [P, PACK], F32)
        nc.gpsimd.dma_start(gb_in[:], gb.rearrange("(p t) o -> p (t o)", t=PACK))
        nc.gpsimd.dma_start(ga_in[:], ga.rearrange("(p t) o -> p (t o)", t=PACK))
        k1_l = load_list("k1_l", k1)
        nc.sync.dma_start(ds_in[:].bitcast(I32)[0:P:8, :], d_scales[0].bitcast(I32))
        offs_l = load_list("offs_l", offs)
        dw_in = load_words("dw_in", d_words, G)
        n3_l = load_list("n3_l", n3)
        n2_l = load_list("n2_l", n2)
        n4_l = load_list("n4_l", n4)
        n1_l = load_list("n1_l", n1)
        n6_l = load_list("n6_l", n6)
        n5_l = load_list("n5_l", n5)

        twice_nonneg = sb("twice_nonneg", [P, PACK], F32)
        sign = sb("sign", [P, PACK], F32)
        sign_16th = sb("sign_16th", [P, PACK], F32)
        gb_abs = sb("gb_abs", [P, PACK], F32)
        ga_signed = sb("ga_signed", [P, PACK], F32)
        nc.gpsimd.tensor_scalar(twice_nonneg[:], gb_in[:], 0.0, 2.0, ALU.is_ge, ALU.mult)
        nc.gpsimd.tensor_scalar(sign[:], twice_nonneg[:], 1.0, -1.0, ALU.mult, ALU.add)
        nc.gpsimd.tensor_tensor(gb_abs[:], gb_in[:], sign[:], ALU.mult)
        nc.gpsimd.tensor_scalar(sign_16th[:], twice_nonneg[:], 0.0625, -0.0625, ALU.mult, ALU.add)
        nc.gpsimd.tensor_tensor(ga_signed[:], ga_in[:], sign_16th[:], ALU.mult)

        x2w = gather("x2w", xw_in, two_l, U32)
        x2s = gather("x2s", xs_in, two_l, U8)
        ww = deal("ww", ww_in, U32)
        ws = deal("ws", ws_in, U8)
        ds_got = gather("ds_got", ds_in, k1_l, U8)
        ds_dealt = deal("ds_dealt", ds_got, U8)
        for q in range(QUADS):
            nc.sync.dma_start(ds_placed[:].bitcast(I32)[32 * q : 32 * q + 4, :],
                              ds_dealt[:].bitcast(I32)[32 * q : 32 * q + 32 : 8, :])
        x1w = gather("x1w", xw_in, offs_l, U32)
        dw_got = gather("dw_got", dw_in, k1_l, U32)
        x1s = gather("x1s", xs_in, offs_l, U8)
        dw = deal("dw", dw_got, U32)

        b_rows = []
        b_banks = []
        b_copy = sb("b_copy", [P, RELU_PLANES, N], F32)
        for t in range(PACK):
            bank = psum.tile([P, N], F32, name=f"b_bank{t}", tag=f"bank{t}")
            cols = slice(P * t, P * (t + 1))
            product(bank[:], ww[:, cols], ws[:, cols], x2w[:], x2s[:])
            row = sb(f"b_row{t}", [P, 2 * N], F32)
            nc.scalar.activation(row[:, 0:N], bank[:], ACT.Copy, scale=gb_abs[:, t : t + 1])
            if t < RELU_PLANES:
                nc.scalar.activation(b_copy[:, t, :], bank[:], ACT.Copy, scale=gb_abs[:, t : t + 1])
            b_rows.append(row)
            b_banks.append(bank)

        above = sb("above", [P, RELU_PLANES, N], F32)
        rise = sb("rise", [P, RELU_PLANES, N], F32)
        at3 = sb("at3", [P, PACK - RELU_PLANES, N], F32)
        larger = sb("larger", [P, PACK, N], F32)
        for t in range(RELU_PLANES):
            nc.vector.tensor_tensor(above[:, t, :], b_rows[t][:].indirect(n3_l[:]), b_copy[:, t, :], ALU.subtract)
        nc.scalar.activation(rise[:], above[:], ACT.Relu)
        nc.gpsimd.tensor_tensor(larger[:, 0:RELU_PLANES, :], b_copy[:], rise[:], ALU.add)
        for t in range(RELU_PLANES, PACK):
            nc.vector.tensor_copy(at3[:, t - RELU_PLANES, :], b_rows[t][:].indirect(n3_l[:]))
        for t in range(RELU_PLANES, PACK):
            nc.vector.scalar_tensor_tensor(larger[:, t, :], b_banks[t][:], gb_abs[:, t : t + 1],
                                           at3[:, t - RELU_PLANES, :], ALU.mult, ALU.max)

        a_rows = []
        a_banks = []
        for t in range(PACK):
            bank = psum.tile([P, N], F32, name=f"a_bank{t}", tag=f"bank{t if t < RELU_PLANES else t + RELU_PLANES}")
            cols = slice(P * t, P * (t + 1))
            product(bank[:], dw[:, cols], ds_placed[:, cols], x1w[:], x1s[:])
            row = sb(f"a_row{t}", [P, 2 * N], F32)
            nc.scalar.copy(row[:, 0:N], bank[:])
            a_rows.append(row)
            a_banks.append(bank)

        at2 = [gather(f"at2_{t}", a_rows[t], n2_l, F32) for t in range(PACK)]
        a_gained = sb("a_gained", [P, PACK, N], F32)
        gate = sb("gate", [P, PACK, N], F32)
        for t in range(PACK):
            diff = sb(f"diff{t}", [P, N], F32)
            nc.vector.tensor_tensor(diff[:], a_rows[t][:].indirect(n1_l[:]), at2[t][:], ALU.subtract)
            nc.scalar.activation(a_gained[:, t, :].rearrange("p (o e m) -> p o e m", e=2, o=2),
                                 a_banks[t][:].rearrange("p (m e o) -> p o e m", e=2, o=2),
                                 ACT.Copy, scale=ga_signed[:, t : t + 1])
            nc.scalar.activation(gate[:, t, :].rearrange("p (o e m) -> p m e o", e=2, o=2),
                                 diff[:].rearrange("p (m e o) -> p m e o", e=2, o=2),
                                 ACT.Sigmoid, scale=0.0625)

        halves = [slice(0, HALF), slice(HALF, N)]
        at4 = sb("at4", [P, 2, PACK, HALF], F32, tag=f"a_row{PACK - 1}")
        for h, cols in enumerate(halves):
            entries = slice(cols.start // GROUP, cols.stop // GROUP)
            for t in range(PACK):
                nc.vector.tensor_copy(at4[:, h, t, :], b_rows[t][:].indirect(n4_l[:, entries]))

        z2_bf = [sb(f"z2_bf{h}", [P, HALF, PACK], BF16) for h in range(2)]
        z2w = sb("z2w", [P, N], U32)
        z2s = sb("z2s", [P, N], U8)
        zw = [sb(f"zw{odd}", [P, HALF], U32) for odd in range(2)]
        zs = [sb(f"zs{odd}", [P, HALF], U8) for odd in range(2)]
        s_rows = [sb(f"s_row{t}", [P, N], F32) for t in range(PACK)]

        def s_product(t, cols, tag):
            bank = psum.tile([P, cols.stop - cols.start], F32, name=f"s_{tag}", tag=tag)
            places = slice(P * (t // 2), P * (t // 2 + 1))
            product(bank[:], zw[t % 2][:, places], zs[t % 2][:, places], z2w[:, cols], z2s[:, cols])
            nc.scalar.activation(s_rows[t][:, cols], bank[:], ACT.Copy, scale=0.0625)

        z_even = sb("z_even", [P, HALF, PACK], BF16)
        z_planes = sb("z_planes", [P, PACK, HALF], BF16)
        nc.gpsimd.tensor_tensor(z_planes[:], a_gained[:, :, halves[0]], gate[:, :, halves[0]], ALU.mult)
        nc.scalar.copy(word_side(z_even[:]), plane_side(z_planes[:]))
        for h, cols in enumerate(halves):
            nc.vector.tensor_tensor(word_side(z2_bf[h][:]), plane_side(larger[:, :, cols]), plane_side(at4[:, h]), ALU.min)
        quantize(z2w[:, halves[0]], z2s[:, halves[0]], z2_bf[0][:])
        quantize(zw[0][:], zs[0][:], z_even[:])
        quantize(z2w[:, halves[1]], z2s[:, halves[1]], z2_bf[1][:])
        for t in (0, 2):
            for h, cols in enumerate(halves):
                s_product(t, cols, f"bank{PACK + t + h}")
        z_odd = sb("z_odd", [P, HALF, PACK], BF16, tag="z_even")
        nc.vector.tensor_tensor(word_side(z_odd[:]), plane_side(a_gained[:, :, halves[1]]),
                                plane_side(gate[:, :, halves[1]]), ALU.mult)
        quantize(zw[1][:], zs[1][:], z_odd[:])
        for t in (3, 1):
            s_product(t, slice(0, N), f"bank{t}")

        out_rows = out_0.rearrange("(p t) v -> p t v", t=PACK)
        y_bf = sb("y_bf", [P, N, PACK], BF16)
        y = [sb(f"y{t}", [P, N], F32) for t in range(PACK)]
        reuse = {3: "both0", LAST: "minus_two_pb0"}
        for pair in ((0, 2), (3, LAST)):
            pb = {t: sb(f"pb{t}", [P, HALF], F32, tag=reuse.get(t)) for t in pair}
            both = {t: sb(f"both{t}", [P, HALF], F32) for t in pair}
            minus_two_pb = {t: sb(f"minus_two_pb{t}", [P, HALF], F32) for t in pair}
            for t in pair:
                nc.vector.tensor_copy(pb[t][:], s_rows[t][:].indirect(n6_l[:]))
                nc.scalar.activation(minus_two_pb[t][:], pb[t][:], ACT.Copy, scale=-2.0)
            for t in pair:
                nc.vector.tensor_tensor(both[t][:], s_rows[t][:].indirect(n5_l[:]), pb[t][:], ALU.add)
            for t in pair:
                nc.vector.tensor_tensor(y[t][:].indirect(n5_l[:]), both[t][:], three_quarters[:], ALU.mult)
            for t in pair:
                nc.vector.tensor_tensor(y[t][:].indirect(n6_l[:]), both[t][:], minus_two_pb[t][:], ALU.add)
                nc.sync.dma_start(out_rows[:, t, :], y[t][:])
                if t != LAST:
                    nc.scalar.copy(y_bf[:, :, t], y[t][:])

        yw = sb("yw", [P, N], U32)
        ys = sb("ys", [P, N], U8)
        for cols in halves:
            nc.vector.tensor_copy(y_bf[:, cols, LAST], y[LAST][:, cols])
        for cols in halves:
            quantize(yw[:, cols], ys[:, cols], y_bf[:, cols, :])
            nc.sync.dma_start(as_words(out_1)[:, cols], yw[:].bitcast(I32)[:, cols])
        for q in range(QUADS):
            queue = nc.scalar if q % 2 == 0 else nc.sync
            queue.dma_start(out_2[0].bitcast(I32)[4 * q : 4 * q + 4, :], ys[:].bitcast(I32)[32 * q : 32 * q + 4, :])
